import numpy as np
import ml_dtypes


def mxq(x, axis, fmt="e4m3"):
    dtype, down = {"e4m3": (ml_dtypes.float8_e4m3fn, 7), "e5m2": (ml_dtypes.float8_e5m2, 14)}[fmt]
    v = np.moveaxis(np.asarray(x, np.float32).astype(ml_dtypes.bfloat16).astype(np.float64), axis, -1)
    blocks = v.reshape(v.shape[:-1] + (-1, 32))
    amax = np.abs(blocks).max(-1, keepdims=True)
    byte = np.maximum(np.where(amax > 0, np.frexp(amax)[1] - 1 + 127, 0) - down, 1)
    scale = np.exp2(byte - 127.0)
    codes = (blocks / scale).astype(np.float32).astype(dtype).astype(np.float64)
    return np.moveaxis((codes * scale).reshape(v.shape), -1, axis)


WIDE = False


def mx_kscale(k):
    if not WIDE:
        return np.ones(k)
    levels = np.array([30, -30])
    if k % 512:
        return np.exp2(np.random.permutation(np.resize(levels, k // 32))).repeat(32)
    a = np.empty((k // 512, 16))
    for p in range(k // 512):
        a[p, :8] = np.random.permutation(np.resize(levels, 8))
        for g in range(8):
            far = levels[np.abs(levels - a[p, g]) >= 10]
            a[p, g + 8] = far[np.random.randint(len(far))]
    return np.exp2(a.ravel()).repeat(32)


def f64(x):
    return np.asarray(x).astype(np.float64)


def striped(idx):
    return np.tile(idx.reshape(-1, 16).T, (8, 1)).astype(np.uint16)


def unstriped(offs):
    return offs[:16].T.reshape(-1).astype(np.int64)


K, T, E, C, N = 512, 1280, 2, 512, 1536


def by_expert(wq, xq):
    return np.concatenate([wq[e].T @ xq[:, e * C:(e + 1) * C] for e in range(E)], axis=1)


def setup_inputs():
    n = np.random.standard_normal
    s = mx_kscale(N)[:, None]
    return {
        "dyT": (n((N, T)) * s).astype(np.float32),
        "w": (n((E, N, K)) / np.sqrt(N) / s[None]).astype(np.float32),
        "gate": np.tile(np.random.uniform(0.2, 1.0, E * C), (N, 1)).astype(np.float32),
        "offs": striped(np.random.permutation(T)[:E * C]),
    }


def reference(dyT, w, gate, offs):
    idx = unstriped(offs)
    gq = mxq(f64(gate) * f64(dyT)[:, idx], 0, "e5m2")
    dx = by_expert(mxq(f64(w), 1, "e4m3"), gq)
    out = np.zeros((K, T))
    out[:, idx] = dx
    return out

@@ -1,0 +1,164 @@
+from contextlib import ExitStack
+
+import concourse.mybir as mybir
+
+F32 = mybir.dt.float32
+BF16 = mybir.dt.bfloat16
+U32 = mybir.dt.uint32
+U16 = mybir.dt.uint16
+U8 = mybir.dt.uint8
+E4M3 = mybir.dt.float8_e4m3fn_x4
+E5M2 = mybir.dt.float8_e5m2_x4
+MULT = mybir.AluOpType.mult
+
+P = 128
+PACK = 4
+N, T, E, C, K = 1536, 1280, 2, 512, 512
+SLOTS = E * C
+PASSES = N // (P * PACK)
+KB = K // P
+LISTED = 16
+
+FLOPS = 2 * SLOTS * N * K
+BYTES = 4 * (N * T + E * N * K + SLOTS + K * T) + 2 * SLOTS
+
+
+def interleave(rows_first):
+    return rows_first.rearrange("p j (c i) -> p c j i", i=4)
+
+
+def tile_moe_bdx_lin_none_kernel(tc, dyT, w, gate, offs, out):
+    nc = tc.nc
+    dy_rows = dyT.rearrange("(g p j) t -> g j p t", p=P, j=PACK)
+    w_rows = w.rearrange("e (g p j) k -> e g p j k", p=P, j=PACK)
+
+    with ExitStack() as ctx:
+        keep = ctx.enter_context(tc.tile_pool(name="keep", bufs=1))
+        raws = ctx.enter_context(tc.tile_pool(name="raws", bufs=3))
+        pairs = ctx.enter_context(tc.tile_pool(name="pairs", bufs=2))
+        sums = ctx.enter_context(tc.tile_pool(name="sums", bufs=4))
+        psum = ctx.enter_context(tc.psum_pool(name="psum", bufs=1))
+
+        offsets = keep.tile([P, SLOTS // LISTED], U16, name="offsets")
+        gates = keep.tile([P, SLOTS], F32, name="gates")
+        dy = {}
+        for g in range(PASSES):
+            for j in range(PACK):
+                dy[g, j] = keep.tile([P, T], F32, name=f"dy{g}{j}")
+        picked = {}
+        for g in range(PASSES):
+            if g < PASSES - 1:
+                both = keep.tile([P, PACK, SLOTS], F32, name=f"picked{g}")
+                for e in range(E):
+                    picked[g, e] = both[:, :, e * C : (e + 1) * C]
+                picked[g] = both[:, :, :]
+            else:
+                for e in range(E):
+                    half = keep.tile([P, PACK, C], F32, name=f"picked{g}{e}")
+                    picked[g, e] = half[:, :, :]
+        placed = [keep.tile([P, T], F32, name=f"placed{m}") for m in range(KB)]
+        acc = {}
+        for e in range(E):
+            for m in range(KB):
+                acc[e, m] = psum.tile([P, C], F32, name=f"acc{e}{m}")
+        w_raw = {}
+        codes = {}
+
+        def load_dy(g, j):
+            nc.sync.dma_start(out=dy[g, j][:], in_=dy_rows[g, j])
+
+        def load_w(g, e):
+            raw = raws.tile([P, PACK, K], F32, name="raw")
+            nc.sync.dma_start(out=raw[:], in_=w_rows[e, g])
+            w_raw[g, e] = raw
+
+        def gather(g, j, e):
+            half = slice(e * C, (e + 1) * C)
+            cols = slice(e * C // LISTED, (e + 1) * C // LISTED)
+            nc.vector.tensor_tensor(picked[g, e][:, j, :], dy[g, j][:].indirect(offsets[:, cols]), gates[:, half], MULT)
+
+        def gather_both(g, j):
+            nc.vector.tensor_tensor(picked[g][:, j, :], dy[g, j][:].indirect(offsets[:]), gates[:], MULT)
+
+        def quantise(what, g, e):
+            if what == "w":
+                source, tag, fmt = w_raw[g, e][:], "w_bf", E4M3
+            else:
+                source, tag, fmt = picked[g, e], "g_bf", E5M2
+            grouped = pairs.tile([P, C, PACK], BF16, name=tag, align_bytes=64)
+            nc.scalar.copy(grouped[:].rearrange("p (c i) j -> p c j i", i=4), interleave(source))
+            words = keep.tile([P, C], U32, name=f"{what}_words{g}{e}", align_bytes=64)
+            scales = keep.tile([P, C], U8, name=f"{what}_scales{g}{e}", align_bytes=64)
+            nc.vector.quantize_mx(out=words[:].bitcast(fmt), scales=scales[:], in_=grouped[:].rearrange("p c j -> p (c j)"))
+            codes[what, g, e] = (words, scales)
+
+        def multiply(g, e):
+            w_words, w_scales = codes["w", g, e]
+            g_words, g_scales = codes["g", g, e]
+            for m in range(KB):
+                cols = slice(m * P, (m + 1) * P)
+                nc.tensor.matmul_mx(
+                    out=acc[e, m][:],
+                    lhsT=w_words[:, cols].bitcast(E4M3),
+                    lhsT_scale=w_scales[:, cols],
+                    rhs=g_words[:].bitcast(E5M2),
+                    rhs_scale=g_scales[:],
+                    start=(g == 0),
+                    stop=(g == PASSES - 1),
+                )
+
+        def scatter(m, e):
+            cols = slice(e * C // LISTED, (e + 1) * C // LISTED)
+            dx = sums.tile([P, C], F32, name="dx")
+            nc.scalar.copy(dx[:], acc[e, m][:])
+            nc.vector.tensor_copy(placed[m][:].indirect(offsets[:, cols]), dx[:])
+
+        nc.sync.dma_start(offsets[:], offs)
+        nc.scalar.dma_start(out=gates[:, 0:C], in_=gate[0:P, 0:C])
+        load_dy(0, 0)
+        nc.scalar.dma_start(out=gates[:, C:SLOTS], in_=gate[0:P, C:SLOTS])
+        for j in range(1, PACK):
+            load_dy(0, j)
+        load_w(0, 0)
+        for j in range(PACK):
+            load_dy(1, j)
+        load_w(1, 0)
+        for j in range(PACK):
+            load_dy(2, j)
+        load_w(2, 0)
+
+        for m in range(KB):
+            (nc.vector if m % 2 else nc.gpsimd).memset(placed[m][:], 0.0)
+
+        for e in range(E):
+            gather(0, 0, e)
+        for j in range(1, PACK):
+            gather_both(0, j)
+        quantise("w", 0, 0)
+        quantise("g", 0, 0)
+        multiply(0, 0)
+        for j in range(PACK):
+            gather_both(1, j)
+        quantise("w", 1, 0)
+        quantise("g", 1, 0)
+        multiply(1, 0)
+        for j in range(PACK):
+            gather(2, j, 0)
+        quantise("w", 2, 0)
+        quantise("g", 2, 0)
+        multiply(2, 0)
+        for j in range(PACK):
+            gather(2, j, 1)
+        for g in range(PASSES):
+            load_w(g, 1)
+        scatter(0, 0)
+        scatter(1, 0)
+        for g in range(PASSES):
+            quantise("g", g, 1)
+            quantise("w", g, 1)
+            multiply(g, 1)
+        scatter(2, 0)
+        scatter(3, 0)
+        for m in range(KB):
+            scatter(m, 1)
+            nc.sync.dma_start(out=out[m * P : (m + 1) * P, :], in_=placed[m][:])

@@ -23,10 +23,6 @@ FLOPS = 2 * SLOTS * N * K
 BYTES = 4 * (N * T + E * N * K + SLOTS + K * T) + 2 * SLOTS
 
 
-def interleave(rows_first):
-    return rows_first.rearrange("p j (c i) -> p c j i", i=4)
-
-
 def tile_moe_bdx_lin_none_kernel(tc, dyT, w, gate, offs, out):
     nc = tc.nc
     dy_rows = dyT.rearrange("(g p j) t -> g j p t", p=P, j=PACK)
@@ -35,7 +31,8 @@ def tile_moe_bdx_lin_none_kernel(tc, dyT, w, gate, offs, out):
     with ExitStack() as ctx:
         keep = ctx.enter_context(tc.tile_pool(name="keep", bufs=1))
         raws = ctx.enter_context(tc.tile_pool(name="raws", bufs=3))
-        pairs = ctx.enter_context(tc.tile_pool(name="pairs", bufs=2))
+        pairs_w = ctx.enter_context(tc.tile_pool(name="pairs_w", bufs=4))
+        pairs_g = ctx.enter_context(tc.tile_pool(name="pairs_g", bufs=5))
         sums = ctx.enter_context(tc.tile_pool(name="sums", bufs=4))
         psum = ctx.enter_context(tc.psum_pool(name="psum", bufs=1))
 
@@ -47,7 +44,7 @@ def tile_moe_bdx_lin_none_kernel(tc, dyT, w, gate, offs, out):
                 dy[g, j] = keep.tile([P, T], F32, name=f"dy{g}{j}")
         picked = {}
         for g in range(PASSES):
-            if g < PASSES - 1:
+            if g < 1:
                 both = keep.tile([P, PACK, SLOTS], F32, name=f"picked{g}")
                 for e in range(E):
                     picked[g, e] = both[:, :, e * C : (e + 1) * C]
@@ -62,7 +59,9 @@ def tile_moe_bdx_lin_none_kernel(tc, dyT, w, gate, offs, out):
             for m in range(KB):
                 acc[e, m] = psum.tile([P, C], F32, name=f"acc{e}{m}")
         w_raw = {}
+        grouped = {}
         codes = {}
+        dx = {}
 
         def load_dy(g, j):
             nc.sync.dma_start(out=dy[g, j][:], in_=dy_rows[g, j])
@@ -80,16 +79,24 @@ def tile_moe_bdx_lin_none_kernel(tc, dyT, w, gate, offs, out):
         def gather_both(g, j):
             nc.vector.tensor_tensor(picked[g][:, j, :], dy[g, j][:].indirect(offsets[:]), gates[:], MULT)
 
+        def cast_w(g, e):
+            pair = pairs_w.tile([P, K, PACK], BF16, name="w_bf", align_bytes=64)
+            nc.scalar.copy(pair[:].rearrange("p (c i) j -> p c j i", i=4), w_raw[g, e][:].rearrange("p j (c i) -> p c j i", i=4))
+            grouped["w", g, e] = pair
+
+        def cast_g(g, e):
+            pair = pairs_g.tile([P, C, PACK], BF16, name="g_bf", align_bytes=64)
+            nc.scalar.copy(pair[:].rearrange("p (c i) j -> p c j i", i=4), picked[g, e].rearrange("p j (c i) -> p c j i", i=4))
+            grouped["g", g, e] = pair
+
         def quantise(what, g, e):
-            if what == "w":
-                source, tag, fmt = w_raw[g, e][:], "w_bf", E4M3
-            else:
-                source, tag, fmt = picked[g, e], "g_bf", E5M2
-            grouped = pairs.tile([P, C, PACK], BF16, name=tag, align_bytes=64)
-            nc.scalar.copy(grouped[:].rearrange("p (c i) j -> p c j i", i=4), interleave(source))
             words = keep.tile([P, C], U32, name=f"{what}_words{g}{e}", align_bytes=64)
             scales = keep.tile([P, C], U8, name=f"{what}_scales{g}{e}", align_bytes=64)
-            nc.vector.quantize_mx(out=words[:].bitcast(fmt), scales=scales[:], in_=grouped[:].rearrange("p c j -> p (c j)"))
+            nc.vector.quantize_mx(
+                out=words[:].bitcast(E4M3 if what == "w" else E5M2),
+                scales=scales[:],
+                in_=grouped[what, g, e][:].rearrange("p c j -> p (c j)"),
+            )
             codes[what, g, e] = (words, scales)
 
         def multiply(g, e):
@@ -107,11 +114,16 @@ def tile_moe_bdx_lin_none_kernel(tc, dyT, w, gate, offs, out):
                     stop=(g == PASSES - 1),
                 )
 
+        def empty(m, e):
+            dx[m, e] = sums.tile([P, C], F32, name="dx")
+            nc.scalar.copy(dx[m, e][:], acc[e, m][:])
+
         def scatter(m, e):
             cols = slice(e * C // LISTED, (e + 1) * C // LISTED)
-            dx = sums.tile([P, C], F32, name="dx")
-            nc.scalar.copy(dx[:], acc[e, m][:])
-            nc.vector.tensor_copy(placed[m][:].indirect(offsets[:, cols]), dx[:])
+            nc.vector.tensor_copy(placed[m][:].indirect(offsets[:, cols]), dx[m, e][:])
+
+        def store(m):
+            nc.sync.dma_start(out=out[m * P : (m + 1) * P, :], in_=placed[m][:])
 
         nc.sync.dma_start(offsets[:], offs)
         nc.scalar.dma_start(out=gates[:, 0:C], in_=gate[0:P, 0:C])
@@ -122,9 +134,11 @@ def tile_moe_bdx_lin_none_kernel(tc, dyT, w, gate, offs, out):
         load_w(0, 0)
         for j in range(PACK):
             load_dy(1, j)
+        load_dy(2, 0)
+        load_dy(2, 1)
         load_w(1, 0)
-        for j in range(PACK):
-            load_dy(2, j)
+        load_dy(2, 2)
+        load_dy(2, 3)
         load_w(2, 0)
 
         for m in range(KB):
@@ -134,31 +148,54 @@ def tile_moe_bdx_lin_none_kernel(tc, dyT, w, gate, offs, out):
             gather(0, 0, e)
         for j in range(1, PACK):
             gather_both(0, j)
+        cast_w(0, 0)
+        load_w(0, 1)
+        cast_g(0, 0)
+        cast_g(0, 1)
+        for j in range(PACK):
+            gather(1, j, 0)
         quantise("w", 0, 0)
         quantise("g", 0, 0)
         multiply(0, 0)
-        for j in range(PACK):
-            gather_both(1, j)
-        quantise("w", 1, 0)
-        quantise("g", 1, 0)
-        multiply(1, 0)
+        cast_g(1, 0)
+        cast_w(1, 0)
+        load_w(1, 1)
         for j in range(PACK):
             gather(2, j, 0)
+        quantise("g", 1, 0)
+        quantise("w", 1, 0)
+        multiply(1, 0)
+        cast_g(2, 0)
+        cast_w(2, 0)
+        load_w(2, 1)
+        for j in range(PACK):
+            gather(1, j, 1)
         quantise("w", 2, 0)
         quantise("g", 2, 0)
         multiply(2, 0)
+        cast_w(0, 1)
+        cast_g(1, 1)
         for j in range(PACK):
             gather(2, j, 1)
-        for g in range(PASSES):
-            load_w(g, 1)
+        for m in range(KB):
+            empty(m, 0)
+        cast_w(1, 1)
+        cast_g(2, 1)
+        cast_w(2, 1)
+        quantise("g", 0, 1)
+        quantise("w", 0, 1)
+        multiply(0, 1)
         scatter(0, 0)
+        quantise("g", 1, 1)
         scatter(1, 0)
-        for g in range(PASSES):
-            quantise("g", g, 1)
-            quantise("w", g, 1)
-            multiply(g, 1)
+        quantise("w", 1, 1)
+        multiply(1, 1)
         scatter(2, 0)
+        quantise("g", 2, 1)
+        quantise("w", 2, 1)
+        multiply(2, 1)
         scatter(3, 0)
         for m in range(KB):
+            empty(m, 1)
             scatter(m, 1)
-            nc.sync.dma_start(out=out[m * P : (m + 1) * P, :], in_=placed[m][:])
+            store(m)

@@ -33,6 +33,7 @@ def tile_moe_bdx_lin_none_kernel(tc, dyT, w, gate, offs, out):
         raws = ctx.enter_context(tc.tile_pool(name="raws", bufs=3))
         pairs_w = ctx.enter_context(tc.tile_pool(name="pairs_w", bufs=4))
         pairs_g = ctx.enter_context(tc.tile_pool(name="pairs_g", bufs=5))
+        picks = ctx.enter_context(tc.tile_pool(name="picks", bufs=3))
         sums = ctx.enter_context(tc.tile_pool(name="sums", bufs=4))
         psum = ctx.enter_context(tc.psum_pool(name="psum", bufs=1))
 
@@ -43,16 +44,6 @@ def tile_moe_bdx_lin_none_kernel(tc, dyT, w, gate, offs, out):
             for j in range(PACK):
                 dy[g, j] = keep.tile([P, T], F32, name=f"dy{g}{j}")
         picked = {}
-        for g in range(PASSES):
-            if g < 1:
-                both = keep.tile([P, PACK, SLOTS], F32, name=f"picked{g}")
-                for e in range(E):
-                    picked[g, e] = both[:, :, e * C : (e + 1) * C]
-                picked[g] = both[:, :, :]
-            else:
-                for e in range(E):
-                    half = keep.tile([P, PACK, C], F32, name=f"picked{g}{e}")
-                    picked[g, e] = half[:, :, :]
         placed = [keep.tile([P, T], F32, name=f"placed{m}") for m in range(KB)]
         acc = {}
         for e in range(E):
@@ -78,6 +69,16 @@ def tile_moe_bdx_lin_none_kernel(tc, dyT, w, gate, offs, out):
 
         def gather_both(g, j):
             nc.vector.tensor_tensor(picked[g][:, j, :], dy[g, j][:].indirect(offsets[:]), gates[:], MULT)
+
+        def room_for_both(g):
+            both = picks.tile([P, PACK, SLOTS], F32, name="pick")
+            picked[g] = both[:, :, :]
+            for e in range(E):
+                picked[g, e] = both[:, :, e * C : (e + 1) * C]
+
+        def room_for_one(g, e):
+            one = picks.tile([P, PACK, C], F32, name="pick")
+            picked[g, e] = one[:, :, :]
 
         def cast_w(g, e):
             pair = pairs_w.tile([P, K, PACK], BF16, name="w_bf", align_bytes=64)
@@ -129,71 +130,75 @@ def tile_moe_bdx_lin_none_kernel(tc, dyT, w, gate, offs, out):
         nc.scalar.dma_start(out=gates[:, 0:C], in_=gate[0:P, 0:C])
         load_dy(0, 0)
         nc.scalar.dma_start(out=gates[:, C:SLOTS], in_=gate[0:P, C:SLOTS])
-        for j in range(1, PACK):
-            load_dy(0, j)
+        load_dy(1, 0)
+        load_dy(0, 1)
         load_w(0, 0)
-        for j in range(PACK):
-            load_dy(1, j)
-        load_dy(2, 0)
-        load_dy(2, 1)
+        load_dy(1, 1)
+        load_dy(0, 2)
         load_w(1, 0)
+        load_dy(1, 2)
+        load_dy(0, 3)
+        load_dy(1, 3)
+        load_dy(2, 0)
+        load_w(2, 0)
+        load_dy(2, 1)
         load_dy(2, 2)
         load_dy(2, 3)
-        load_w(2, 0)
 
         for m in range(KB):
             (nc.vector if m % 2 else nc.gpsimd).memset(placed[m][:], 0.0)
 
-        for e in range(E):
-            gather(0, 0, e)
+        room_for_both(0)
+        room_for_both(1)
+        room_for_one(2, 0)
+        gather(0, 0, 0)
+        gather(0, 0, 1)
+        gather_both(1, 0)
         for j in range(1, PACK):
             gather_both(0, j)
+            gather_both(1, j)
+        for j in range(PACK):
+            gather(2, j, 0)
         cast_w(0, 0)
         load_w(0, 1)
+        cast_w(1, 0)
+        load_w(1, 1)
         cast_g(0, 0)
+        cast_g(1, 0)
+        cast_w(2, 0)
+        load_w(2, 1)
         cast_g(0, 1)
-        for j in range(PACK):
-            gather(1, j, 0)
+        cast_g(2, 0)
+        cast_g(1, 1)
         quantise("w", 0, 0)
         quantise("g", 0, 0)
         multiply(0, 0)
-        cast_g(1, 0)
-        cast_w(1, 0)
-        load_w(1, 1)
-        for j in range(PACK):
-            gather(2, j, 0)
-        quantise("g", 1, 0)
         quantise("w", 1, 0)
+        quantise("g", 1, 0)
         multiply(1, 0)
-        cast_g(2, 0)
-        cast_w(2, 0)
-        load_w(2, 1)
+        room_for_one(2, 1)
         for j in range(PACK):
-            gather(1, j, 1)
+            gather(2, j, 1)
         quantise("w", 2, 0)
         quantise("g", 2, 0)
         multiply(2, 0)
-        cast_w(0, 1)
-        cast_g(1, 1)
-        for j in range(PACK):
-            gather(2, j, 1)
-        for m in range(KB):
+        quantise("g", 0, 1)
+        quantise("g", 1, 1)
+        for m in range(2):
             empty(m, 0)
-        cast_w(1, 1)
+            scatter(m, 0)
+        for g in range(2):
+            cast_w(g, 1)
+            quantise("w", g, 1)
+            multiply(g, 1)
+        empty(2, 0)
+        scatter(2, 0)
         cast_g(2, 1)
         cast_w(2, 1)
-        quantise("g", 0, 1)
-        quantise("w", 0, 1)
-        multiply(0, 1)
-        scatter(0, 0)
-        quantise("g", 1, 1)
-        scatter(1, 0)
-        quantise("w", 1, 1)
-        multiply(1, 1)
-        scatter(2, 0)
         quantise("g", 2, 1)
         quantise("w", 2, 1)
         multiply(2, 1)
+        empty(3, 0)
         scatter(3, 0)
         for m in range(KB):
             empty(m, 1)

@@ -132,18 +132,19 @@ def tile_moe_bdx_lin_none_kernel(tc, dyT, w, gate, offs, out):
         nc.scalar.dma_start(out=gates[:, C:SLOTS], in_=gate[0:P, C:SLOTS])
         load_dy(1, 0)
         load_dy(0, 1)
-        load_w(0, 0)
         load_dy(1, 1)
+        load_w(0, 0)
         load_dy(0, 2)
-        load_w(1, 0)
         load_dy(1, 2)
-        load_dy(0, 3)
-        load_dy(1, 3)
+        load_w(1, 0)
         load_dy(2, 0)
         load_w(2, 0)
+        load_dy(0, 3)
+        load_dy(1, 3)
         load_dy(2, 1)
         load_dy(2, 2)
         load_dy(2, 3)
+        load_w(0, 1)
 
         for m in range(KB):
             (nc.vector if m % 2 else nc.gpsimd).memset(placed[m][:], 0.0)
@@ -154,19 +155,23 @@ def tile_moe_bdx_lin_none_kernel(tc, dyT, w, gate, offs, out):
         gather(0, 0, 0)
         gather(0, 0, 1)
         gather_both(1, 0)
-        for j in range(1, PACK):
-            gather_both(0, j)
-            gather_both(1, j)
-        for j in range(PACK):
-            gather(2, j, 0)
+        gather_both(0, 1)
+        gather_both(1, 1)
+        gather_both(0, 2)
+        gather_both(1, 2)
+        gather(2, 0, 0)
+        gather_both(0, 3)
+        gather_both(1, 3)
+        gather(2, 1, 0)
+        gather(2, 2, 0)
+        gather(2, 3, 0)
         cast_w(0, 0)
-        load_w(0, 1)
-        cast_w(1, 0)
         load_w(1, 1)
-        cast_g(0, 0)
-        cast_g(1, 0)
-        cast_w(2, 0)
+        cast_w(1, 0)
         load_w(2, 1)
+        cast_g(0, 0)
+        cast_w(2, 0)
+        cast_g(1, 0)
         cast_g(0, 1)
         cast_g(2, 0)
         cast_g(1, 1)

@@ -127,9 +127,9 @@ def tile_moe_bdx_lin_none_kernel(tc, dyT, w, gate, offs, out):
             nc.sync.dma_start(out=out[m * P : (m + 1) * P, :], in_=placed[m][:])
 
         nc.sync.dma_start(offsets[:], offs)
-        nc.scalar.dma_start(out=gates[:, 0:C], in_=gate[0:P, 0:C])
+        nc.sync.dma_start(out=gates[:, 0:C], in_=gate[0:P, 0:C])
         load_dy(0, 0)
-        nc.scalar.dma_start(out=gates[:, C:SLOTS], in_=gate[0:P, C:SLOTS])
+        nc.sync.dma_start(out=gates[:, C:SLOTS], in_=gate[0:P, C:SLOTS])
         load_dy(1, 0)
         load_dy(0, 1)
         load_dy(1, 1)

from contextlib import ExitStack

import concourse.mybir as mybir

F32 = mybir.dt.float32
BF16 = mybir.dt.bfloat16
U32 = mybir.dt.uint32
U16 = mybir.dt.uint16
U8 = mybir.dt.uint8
E4M3 = mybir.dt.float8_e4m3fn_x4
E5M2 = mybir.dt.float8_e5m2_x4
MULT = mybir.AluOpType.mult

P = 128
PACK = 4
N, T, E, C, K = 1536, 1280, 2, 512, 512
SLOTS = E * C
PASSES = N // (P * PACK)
KB = K // P
LISTED = 16

FLOPS = 2 * SLOTS * N * K
BYTES = 4 * (N * T + E * N * K + SLOTS + K * T) + 2 * SLOTS


def tile_moe_bdx_lin_none_kernel(tc, dyT, w, gate, offs, out):
    nc = tc.nc
    dy_rows = dyT.rearrange("(g p j) t -> g j p t", p=P, j=PACK)
    w_rows = w.rearrange("e (g p j) k -> e g p j k", p=P, j=PACK)

    with ExitStack() as ctx:
        keep = ctx.enter_context(tc.tile_pool(name="keep", bufs=1))
        raws = ctx.enter_context(tc.tile_pool(name="raws", bufs=3))
        pairs_w = ctx.enter_context(tc.tile_pool(name="pairs_w", bufs=4))
        pairs_g = ctx.enter_context(tc.tile_pool(name="pairs_g", bufs=5))
        picks = ctx.enter_context(tc.tile_pool(name="picks", bufs=3))
        sums = ctx.enter_context(tc.tile_pool(name="sums", bufs=4))
        psum = ctx.enter_context(tc.psum_pool(name="psum", bufs=1))

        offsets = keep.tile([P, SLOTS // LISTED], U16, name="offsets")
        gates = keep.tile([P, SLOTS], F32, name="gates")
        dy = {}
        for g in range(PASSES):
            for j in range(PACK):
                dy[g, j] = keep.tile([P, T], F32, name=f"dy{g}{j}")
        picked = {}
        placed = [keep.tile([P, T], F32, name=f"placed{m}") for m in range(KB)]
        acc = {}
        for e in range(E):
            for m in range(KB):
                acc[e, m] = psum.tile([P, C], F32, name=f"acc{e}{m}")
        w_raw = {}
        grouped = {}
        codes = {}
        dx = {}

        def load_dy(g, j):
            nc.sync.dma_start(out=dy[g, j][:], in_=dy_rows[g, j])

        def load_w(g, e):
            raw = raws.tile([P, PACK, K], F32, name="raw")
            nc.sync.dma_start(out=raw[:], in_=w_rows[e, g])
            w_raw[g, e] = raw

        def gather(g, j, e):
            half = slice(e * C, (e + 1) * C)
            cols = slice(e * C // LISTED, (e + 1) * C // LISTED)
            nc.vector.tensor_tensor(picked[g, e][:, j, :], dy[g, j][:].indirect(offsets[:, cols]), gates[:, half], MULT)

        def gather_both(g, j):
            nc.vector.tensor_tensor(picked[g][:, j, :], dy[g, j][:].indirect(offsets[:]), gates[:], MULT)

        def room_for_both(g):
            both = picks.tile([P, PACK, SLOTS], F32, name="pick")
            picked[g] = both[:, :, :]
            for e in range(E):
                picked[g, e] = both[:, :, e * C : (e + 1) * C]

        def room_for_one(g, e):
            one = picks.tile([P, PACK, C], F32, name="pick")
            picked[g, e] = one[:, :, :]

        def cast_w(g, e):
            pair = pairs_w.tile([P, K, PACK], BF16, name="w_bf", align_bytes=64)
            nc.scalar.copy(pair[:].rearrange("p (c i) j -> p c j i", i=4), w_raw[g, e][:].rearrange("p j (c i) -> p c j i", i=4))
            grouped["w", g, e] = pair

        def cast_g(g, e):
            pair = pairs_g.tile([P, C, PACK], BF16, name="g_bf", align_bytes=64)
            nc.scalar.copy(pair[:].rearrange("p (c i) j -> p c j i", i=4), picked[g, e].rearrange("p j (c i) -> p c j i", i=4))
            grouped["g", g, e] = pair

        def quantise(what, g, e):
            words = keep.tile([P, C], U32, name=f"{what}_words{g}{e}", align_bytes=64)
            scales = keep.tile([P, C], U8, name=f"{what}_scales{g}{e}", align_bytes=64)
            nc.vector.quantize_mx(
                out=words[:].bitcast(E4M3 if what == "w" else E5M2),
                scales=scales[:],
                in_=grouped[what, g, e][:].rearrange("p c j -> p (c j)"),
            )
            codes[what, g, e] = (words, scales)

        def multiply(g, e):
            w_words, w_scales = codes["w", g, e]
            g_words, g_scales = codes["g", g, e]
            for m in range(KB):
                cols = slice(m * P, (m + 1) * P)
                nc.tensor.matmul_mx(
                    out=acc[e, m][:],
                    lhsT=w_words[:, cols].bitcast(E4M3),
                    lhsT_scale=w_scales[:, cols],
                    rhs=g_words[:].bitcast(E5M2),
                    rhs_scale=g_scales[:],
                    start=(g == 0),
                    stop=(g == PASSES - 1),
                )

        def empty(m, e):
            dx[m, e] = sums.tile([P, C], F32, name="dx")
            nc.scalar.copy(dx[m, e][:], acc[e, m][:])

        def scatter(m, e):
            cols = slice(e * C // LISTED, (e + 1) * C // LISTED)
            nc.vector.tensor_copy(placed[m][:].indirect(offsets[:, cols]), dx[m, e][:])

        def store(m):
            nc.sync.dma_start(out=out[m * P : (m + 1) * P, :], in_=placed[m][:])

        nc.sync.dma_start(offsets[:], offs)
        nc.sync.dma_start(out=gates[:, 0:C], in_=gate[0:P, 0:C])
        load_dy(0, 0)
        nc.sync.dma_start(out=gates[:, C:SLOTS], in_=gate[0:P, C:SLOTS])
        load_dy(1, 0)
        load_dy(0, 1)
        load_dy(1, 1)
        load_w(0, 0)
        load_dy(0, 2)
        load_dy(1, 2)
        load_w(1, 0)
        load_dy(2, 0)
        load_w(2, 0)
        load_dy(0, 3)
        load_dy(1, 3)
        load_dy(2, 1)
        load_dy(2, 2)
        load_dy(2, 3)
        load_w(0, 1)

        for m in range(KB):
            (nc.vector if m % 2 else nc.gpsimd).memset(placed[m][:], 0.0)

        room_for_both(0)
        room_for_both(1)
        room_for_one(2, 0)
        gather(0, 0, 0)
        gather(0, 0, 1)
        gather_both(1, 0)
        gather_both(0, 1)
        gather_both(1, 1)
        gather_both(0, 2)
        gather_both(1, 2)
        gather(2, 0, 0)
        gather_both(0, 3)
        gather_both(1, 3)
        gather(2, 1, 0)
        gather(2, 2, 0)
        gather(2, 3, 0)
        cast_w(0, 0)
        load_w(1, 1)
        cast_w(1, 0)
        load_w(2, 1)
        cast_g(0, 0)
        cast_w(2, 0)
        cast_g(1, 0)
        cast_g(0, 1)
        cast_g(2, 0)
        cast_g(1, 1)
        quantise("w", 0, 0)
        quantise("g", 0, 0)
        multiply(0, 0)
        quantise("w", 1, 0)
        quantise("g", 1, 0)
        multiply(1, 0)
        room_for_one(2, 1)
        for j in range(PACK):
            gather(2, j, 1)
        quantise("w", 2, 0)
        quantise("g", 2, 0)
        multiply(2, 0)
        quantise("g", 0, 1)
        quantise("g", 1, 1)
        for m in range(2):
            empty(m, 0)
            scatter(m, 0)
        for g in range(2):
            cast_w(g, 1)
            quantise("w", g, 1)
            multiply(g, 1)
        empty(2, 0)
        scatter(2, 0)
        cast_g(2, 1)
        cast_w(2, 1)
        quantise("g", 2, 1)
        quantise("w", 2, 1)
        multiply(2, 1)
        empty(3, 0)
        scatter(3, 0)
        for m in range(KB):
            empty(m, 1)
            scatter(m, 1)
            store(m)
